import numpy as np
import ml_dtypes


def mxq(x, axis, fmt="e4m3"):
    dtype, down = {"e4m3": (ml_dtypes.float8_e4m3fn, 7), "e5m2": (ml_dtypes.float8_e5m2, 14)}[fmt]
    v = np.moveaxis(np.asarray(x, np.float32).astype(ml_dtypes.bfloat16).astype(np.float64), axis, -1)
    blocks = v.reshape(v.shape[:-1] + (-1, 32))
    amax = np.abs(blocks).max(-1, keepdims=True)
    byte = np.maximum(np.where(amax > 0, np.frexp(amax)[1] - 1 + 127, 0) - down, 1)
    scale = np.exp2(byte - 127.0)
    codes = (blocks / scale).astype(np.float32).astype(dtype).astype(np.float64)
    return np.moveaxis((codes * scale).reshape(v.shape), -1, axis)


WIDE = False


def mx_kscale(k):
    if not WIDE:
        return np.ones(k)
    levels = np.array([10, -10, 5, -5, 0])
    if k % 512:
        return np.exp2(np.random.permutation(np.resize(levels, k // 32))).repeat(32)
    a = np.empty((k // 512, 16))
    for p in range(k // 512):
        a[p, :8] = np.random.permutation(np.resize(levels, 8))
        for g in range(8):
            far = levels[np.abs(levels - a[p, g]) >= 10]
            a[p, g + 8] = far[np.random.randint(len(far))]
    return np.exp2(a.ravel()).repeat(32)


def f64(x):
    return np.asarray(x).astype(np.float64)


def striped(idx):
    return np.tile(idx.reshape(-1, 16).T, (8, 1)).astype(np.uint16)


def unstriped(offs):
    return offs[:16].T.reshape(-1).astype(np.int64)


def pack_weight(w):
    k, n = w.shape
    w = f64(np.asarray(w, np.float32).astype(ml_dtypes.bfloat16)).reshape(k // 32, 32, n)
    amax = np.abs(w).max(1)
    byte = np.clip(np.where(amax > 0, np.frexp(amax)[1] - 1 + 127 - 7, 1), 1, 254)
    scaled = (w * np.exp2(127.0 - byte)[:, None, :]).reshape(k, n).astype(np.float32)
    words = np.ascontiguousarray(scaled.reshape(k // 512, 128, 4, n).transpose(0, 1, 3, 2)).astype(ml_dtypes.float8_e4m3fn).view(np.uint8)
    return words, np.ascontiguousarray(byte.astype(np.uint8).reshape(k // 512, 16, n))


def unpack_weight(words, scales):
    g, p, n, _ = words.shape
    vals = np.ascontiguousarray(words).view(ml_dtypes.float8_e4m3fn).astype(np.float64) * np.repeat(np.exp2(scales.astype(np.float64) - 127.0), 8, axis=1)[..., None]
    return vals.transpose(0, 1, 3, 2).reshape(g * 512, n)


K, T, E, C, N = 2048, 384, 12, 128, 256
TOP = 4


def by_expert(wq, xq):
    return np.concatenate([wq[e].T @ xq[:, e * C:(e + 1) * C] for e in range(E)], axis=1)


def setup_inputs():
    n = np.random.standard_normal
    s = mx_kscale(K)[:, None]
    deal = np.repeat(np.arange(E), C).reshape(TOP, T)[:, np.random.permutation(T)]
    deal = np.take_along_axis(deal, np.argsort(np.random.rand(TOP, T), axis=0), axis=0)
    for _ in range(8):
        s_, t_ = np.random.permutation(T).reshape(2, -1); r = np.random.randint(TOP, size=T // 2); x, y = deal[r, s_].copy(), deal[r, t_].copy()
        ok = ~((deal[:, s_] == y).any(0) | (deal[:, t_] == x).any(0)); deal[r[ok], s_[ok]] = y[ok]; deal[r[ok], t_[ok]] = x[ok]
    order = np.lexsort((np.random.rand(TOP * T), deal.reshape(-1)))
    slot_token = order % T; pos = np.empty(TOP * T, np.int64); pos[order] = np.arange(TOP * T); pos = pos.reshape(TOP, T)
    g = np.random.uniform(0.5, 1.5, (TOP, T)); g = g / g.sum(0)
    packed = [pack_weight(m) for m in n((E, K, N)) / np.sqrt(K) / s[None]]
    return {
        "xT": (n((K, T)) * s).astype(np.float32),
        "w_words": np.stack([m[0] for m in packed]),
        "w_scales": np.stack([m[1] for m in packed]),
        "b": (0.3 * n((N, E))).astype(np.float32),
        "gate": np.stack([np.tile(r, (N, 1)) for r in g]).astype(np.float32),
        "offs": striped(slot_token),
        "pos1": striped(pos[0]),
        "pos2": striped(pos[1]),
        "pos3": striped(pos[2]),
        "pos4": striped(pos[3]),
    }


def reference(xT, w_words, w_scales, b, gate, offs, pos1, pos2, pos3, pos4):
    idx = unstriped(offs)
    w = np.stack([unpack_weight(w_words[e], w_scales[e]) for e in range(E)])
    xq = mxq(f64(xT)[:, idx], 0, "e4m3")
    y = by_expert(w, xq)
    y = y + np.repeat(f64(b), C, axis=1)
    return sum(f64(gate[r]) * y[:, unstriped(p)] for r, p in enumerate((pos1, pos2, pos3, pos4)))

@@ -1,0 +1,193 @@
+from contextlib import ExitStack
+
+import concourse.mybir as mybir
+
+K, T, E, C, N, R = 2048, 384, 12, 128, 256, 4
+S = E * C
+P = 128
+PASSES = 4
+HALVES = 2
+WINDOW = 1024
+
+FLOPS = 2 * S * K * N
+BYTES = 4 * K * T + E * K * N + E * K * N // 32 + 4 * N * E + 4 * R * P * T + 2 * P * (S + R * T) // 16 + 4 * N * T
+
+F32 = mybir.dt.float32
+BF16 = mybir.dt.bfloat16
+U32 = mybir.dt.uint32
+I32 = mybir.dt.int32
+U16 = mybir.dt.uint16
+U8 = mybir.dt.uint8
+FP8X4 = mybir.dt.float8_e4m3fn_x4
+
+IDENT = mybir.ActivationFunctionType.Identity
+MULT = mybir.AluOpType.mult
+ADD = mybir.AluOpType.add
+
+CHUNKS = ((0, 3), (3, 6), (6, 9), (9, 11), (11, 12))
+SPLIT_FROM = 8
+
+
+def tile_moe_tk_lin_bias_kernel(tc, xT, w_words, w_scales, b, gate, offs, pos1, pos2, pos3, pos4, out):
+    nc = tc.nc
+    with ExitStack() as ctx:
+        keep = ctx.enter_context(tc.tile_pool(name="keep", bufs=1))
+        psum = ctx.enter_context(tc.psum_pool(name="psum", bufs=1))
+
+        x_parts = []
+        for a in range(PASSES):
+            cuts = ((0, 256), (256, 384)) if a == 0 else ((0, T),)
+            parts = []
+            for t0, t1 in cuts:
+                raw = keep.tile([P, 4, t1 - t0], F32, name=f"raw{a}_{t0}")
+                nc.sync.dma_start(out=raw[:], in_=xT[512 * a : 512 * (a + 1), t0:t1].rearrange("(p j) t -> p j t", j=4))
+                parts.append((t0, t1, raw))
+            x_parts.append(parts)
+            if a == 0:
+                offs_t = keep.tile([P, S // 16], U16, name="offs_t")
+                nc.sync.dma_start(out=offs_t[:], in_=offs)
+
+        ws = keep.tile([P, E * N], U8, name="ws", align_bytes=64)
+        nc.gpsimd.memset(ws[:].bitcast(I32), 0)
+        for q in range(4):
+            for a in range(PASSES):
+                row = 32 * q + 4 * a
+                nc.gpsimd.dma_start(
+                    out=ws[row : row + 4, :].rearrange("r (e n) -> r e n", e=E).bitcast(I32),
+                    in_=w_scales[:, a, 4 * q : 4 * q + 4, :].rearrange("e r n -> r e n").bitcast(I32),
+                )
+
+        b_t = keep.tile([P, HALVES, E], F32, name="b_t")
+        nc.scalar.dma_start(out=b_t[:], in_=b.rearrange("(h p) e -> p h e", h=HALVES))
+
+        w_t = []
+        for e in range(E):
+            w_t.append(keep.tile([P, PASSES * N], U32, name=f"w{e}", align_bytes=64))
+
+        def load_w(e, n0, n1):
+            nc.sync.dma_start(
+                out=w_t[e][:].rearrange("p (a n) -> p a n", a=PASSES)[:, :, n0:n1].bitcast(I32),
+                in_=w_words[e].rearrange("a p n r -> p a (n r)")[:, :, 4 * n0 : 4 * n1].bitcast(I32),
+            )
+
+        for e in range(SPLIT_FROM):
+            load_w(e, 0, N)
+        pos_t = []
+        for r, pos in enumerate((pos1, pos2, pos3, pos4)):
+            tile = keep.tile([P, T // 16], U16, name=f"pos_t{r}")
+            nc.sync.dma_start(out=tile[:], in_=pos)
+            pos_t.append(tile)
+        gate_t = keep.tile([P, R, T], F32, name="gate_t")
+        nc.sync.dma_start(out=gate_t[:], in_=gate[:, 0:P, :].rearrange("r p t -> p r t"))
+        for h in range(HALVES):
+            for e in range(SPLIT_FROM, E):
+                load_w(e, h * P, (h + 1) * P)
+
+        warm = keep.tile([P, 1], F32, name="warm")
+        warm_out = keep.tile([P, 1], F32, name="warm_out")
+        nc.vector.memset(warm[:], 0.0)
+        nc.scalar.activation(out=warm_out[:], in_=warm[:], func=IDENT)
+
+        codes = []
+        for a in range(PASSES):
+            codes.append(keep.tile([P, WINDOW], U32, name=f"codes{a}", align_bytes=64))
+            nc.vector.memset(codes[a][:, T:WINDOW].bitcast(I32), 0)
+        scales = keep.tile([P, WINDOW], U8, name="scales", align_bytes=64)
+        nc.gpsimd.memset(scales[:], 0)
+
+        slot_codes = []
+        for a in range(PASSES):
+            slot_codes.append(keep.tile([P, S], U32, name=f"slot_codes{a}", align_bytes=64))
+        slot_scales = keep.tile([P, S], U8, name="slot_scales", align_bytes=64)
+
+        grouped = []
+        for a in range(PASSES):
+            grouped.append(keep.tile([P, T, 4], BF16, name=f"grouped{a}", align_bytes=64))
+
+        def cast(engine_copy, a, t0, t1):
+            for p0, p1, raw in x_parts[a]:
+                if p0 <= t0 and t1 <= p1:
+                    engine_copy(out=grouped[a][:, t0:t1, :], in_=raw[:, :, t0 - p0 : t1 - p0].rearrange("p j t -> p t j"))
+
+        def quantise(a):
+            for t0, t1 in ((0, 256), (256, 384)):
+                nc.vector.quantize_mx(
+                    out=codes[a][:, t0:t1].bitcast(FP8X4),
+                    scales=scales[4 * a : P, t0:t1],
+                    in_=grouped[a][:, t0:t1, :].rearrange("p t j -> p (t j)"),
+                )
+
+        def gather(dst, src, s0, s1):
+            nc.vector.tensor_copy(dst[:, s0:s1], src[:].indirect(offs_t[:, s0 // 16 : s1 // 16]))
+
+        cast(nc.vector.tensor_copy, 0, 0, 128)
+        cast(nc.scalar.copy, 0, 128, 256)
+        cast(nc.vector.tensor_copy, 0, 256, 384)
+        for a in range(1, PASSES):
+            cast(nc.scalar.copy, a, 0, T)
+        for a in (0, 1):
+            quantise(a)
+            gather(slot_codes[a], codes[a], 0, S // 2)
+            gather(slot_codes[a], codes[a], S // 2, S)
+        quantise(2)
+        quantise(3)
+        gather(slot_scales, scales, 0, S // 2)
+        gather(slot_scales, scales, S // 2, S)
+
+        y = []
+        for h in range(HALVES):
+            y.append(keep.tile([P, S], F32, name=f"y{h}"))
+        bank0 = []
+        for c in range(len(CHUNKS)):
+            bank0.append(psum.tile([P, 512], F32, name=f"bank0_{c}"))
+        bank1 = []
+        for c in range(3):
+            bank1.append(psum.tile([P, 512], F32, name=f"bank1_{c}"))
+
+        def multiply(e, h, bank, col):
+            for a in range(PASSES):
+                n0 = a * N + h * P
+                nc.tensor.matmul_mx(
+                    out=bank[:, col : col + C],
+                    lhsT=w_t[e][:, n0 : n0 + P].bitcast(FP8X4),
+                    lhsT_scale=ws[4 * a : P, e * N + h * P : e * N + (h + 1) * P],
+                    rhs=slot_codes[a][:, e * C : (e + 1) * C].bitcast(FP8X4),
+                    rhs_scale=slot_scales[4 * a : P, e * C : (e + 1) * C],
+                    start=(a == 0),
+                    stop=(a == PASSES - 1),
+                )
+
+        def take_out(e, h, bank, col):
+            nc.scalar.activation(out=y[h][:, e * C : (e + 1) * C], in_=bank[:, col : col + C], func=IDENT, bias=b_t[:, h, e : e + 1])
+
+        for c, (e0, e1) in enumerate(CHUNKS):
+            for a in (2, 3):
+                gather(slot_codes[a], codes[a], e0 * C, e1 * C)
+            for e in range(e0, e1):
+                multiply(e, 0, bank0[c], (e - e0) * C)
+            for e in range(e0, e1):
+                take_out(e, 0, bank0[c], (e - e0) * C)
+            for e in range(e0, e1):
+                multiply(e, 1, bank1[e // 4], (e % 4) * C)
+                if e % 4 == 3:
+                    for f in range(e - 3, e + 1):
+                        take_out(f, 1, bank1[f // 4], (f % 4) * C)
+
+        prod = []
+        for h in range(HALVES):
+            prod.append(keep.tile([P, R, T], F32, name=f"prod{h}"))
+
+        def fetch(h, r):
+            nc.vector.tensor_tensor(prod[h][:, r, :], y[h][:].indirect(pos_t[r][:]), gate_t[:, r, :], MULT)
+
+        pair, res = [], []
+        for h in range(HALVES):
+            pair.append(keep.tile([P, 2, T], F32, name=f"pair{h}"))
+            res.append(keep.tile([P, T], F32, name=f"res{h}"))
+        for h in range(HALVES):
+            for r in range(R):
+                fetch(h, r)
+            for u in range(2):
+                nc.vector.tensor_tensor(out=pair[h][:, u, :], in0=prod[h][:, 2 * u, :], in1=prod[h][:, 2 * u + 1, :], op=ADD)
+            nc.vector.tensor_tensor(out=res[h][:], in0=pair[h][:, 0, :], in1=pair[h][:, 1, :], op=ADD)
+            nc.sync.dma_start(out=out[h * P : (h + 1) * P, :], in_=res[h][:])

@@ -1,16 +1,17 @@
 from contextlib import ExitStack
 
 import concourse.mybir as mybir
+from concourse.masks import make_identity
 
 K, T, E, C, N, R = 2048, 384, 12, 128, 256, 4
 S = E * C
 P = 128
 PASSES = 4
 HALVES = 2
-WINDOW = 1024
+WINDOW = 2048
 
 FLOPS = 2 * S * K * N
-BYTES = 4 * K * T + E * K * N + E * K * N // 32 + 4 * N * E + 4 * R * P * T + 2 * P * (S + R * T) // 16 + 4 * N * T
+BYTES = 4 * K * T + E * K * N + E * K * N // 32 + 4 * N * E + 4 * R * T + 2 * P * (S + R * T) // 16 + 4 * N * T
 
 F32 = mybir.dt.float32
 BF16 = mybir.dt.bfloat16
@@ -24,8 +25,8 @@ IDENT = mybir.ActivationFunctionType.Identity
 MULT = mybir.AluOpType.mult
 ADD = mybir.AluOpType.add
 
+SECOND = ((), (), (), (), (0, 1, 2, 3, 4, 5, 6, 7, 8, 9, 10, 11))
 CHUNKS = ((0, 3), (3, 6), (6, 9), (9, 11), (11, 12))
-SPLIT_FROM = 8
 
 
 def tile_moe_tk_lin_bias_kernel(tc, xT, w_words, w_scales, b, gate, offs, pos1, pos2, pos3, pos4, out):
@@ -34,66 +35,83 @@ def tile_moe_tk_lin_bias_kernel(tc, xT, w_words, w_scales, b, gate, offs, pos1, 
         keep = ctx.enter_context(tc.tile_pool(name="keep", bufs=1))
         psum = ctx.enter_context(tc.psum_pool(name="psum", bufs=1))
 
+        warm = keep.tile([P, 1], F32, name="warm")
+        warm_out = keep.tile([P, 1], F32, name="warm_out")
+        nc.vector.memset(warm[:], 0.0)
+        nc.scalar.activation(out=warm_out[:], in_=warm[:], func=IDENT)
+        ws = keep.tile([P, E * N], U8, name="ws", align_bytes=64)
+        nc.vector.memset(ws[:].bitcast(I32), 0)
+        gate_rows = keep.tile([P, T], F32, name="gate_rows")
+        nc.gpsimd.memset(gate_rows[:], 0.0)
+        nc.gpsimd.dma_start(out=gate_rows[0:R, :], in_=gate[:, 0, :])
+        ident = keep.tile([P, P], F32, name="ident")
+        make_identity(nc, ident[:])
+
         x_parts = []
         for a in range(PASSES):
-            cuts = ((0, 256), (256, 384)) if a == 0 else ((0, T),)
-            parts = []
-            for t0, t1 in cuts:
-                raw = keep.tile([P, 4, t1 - t0], F32, name=f"raw{a}_{t0}")
-                nc.sync.dma_start(out=raw[:], in_=xT[512 * a : 512 * (a + 1), t0:t1].rearrange("(p j) t -> p j t", j=4))
-                parts.append((t0, t1, raw))
-            x_parts.append(parts)
-            if a == 0:
-                offs_t = keep.tile([P, S // 16], U16, name="offs_t")
-                nc.sync.dma_start(out=offs_t[:], in_=offs)
+            x_parts.append([])
 
-        ws = keep.tile([P, E * N], U8, name="ws", align_bytes=64)
-        nc.gpsimd.memset(ws[:].bitcast(I32), 0)
+        def load_x(a, t0, t1):
+            raw = keep.tile([P, 4, t1 - t0], F32, name=f"raw{a}_{t0}")
+            nc.sync.dma_start(out=raw[:], in_=xT[512 * a : 512 * (a + 1), t0:t1].rearrange("(p j) t -> p j t", j=4))
+            x_parts[a].append((t0, t1, raw))
+
+        small = []
         for q in range(4):
             for a in range(PASSES):
+                small.append((q, a))
+
+        def load_ws(count):
+            for u in range(count):
+                q, a = small.pop(0)
                 row = 32 * q + 4 * a
-                nc.gpsimd.dma_start(
+                nc.sync.dma_start(
                     out=ws[row : row + 4, :].rearrange("r (e n) -> r e n", e=E).bitcast(I32),
                     in_=w_scales[:, a, 4 * q : 4 * q + 4, :].rearrange("e r n -> r e n").bitcast(I32),
                 )
 
-        b_t = keep.tile([P, HALVES, E], F32, name="b_t")
-        nc.scalar.dma_start(out=b_t[:], in_=b.rearrange("(h p) e -> p h e", h=HALVES))
-
         w_t = []
-        for e in range(E):
-            w_t.append(keep.tile([P, PASSES * N], U32, name=f"w{e}", align_bytes=64))
+        for g in range(E // 2):
+            w_t.append(keep.tile([P, 2 * PASSES * N], U32, name=f"w{g}", align_bytes=64))
 
-        def load_w(e, n0, n1):
+        def load_w(g, n0, n1):
             nc.sync.dma_start(
-                out=w_t[e][:].rearrange("p (a n) -> p a n", a=PASSES)[:, :, n0:n1].bitcast(I32),
-                in_=w_words[e].rearrange("a p n r -> p a (n r)")[:, :, 4 * n0 : 4 * n1].bitcast(I32),
+                out=w_t[g][:].rearrange("p (a n) -> p a n", a=2 * PASSES)[:, :, n0:n1].bitcast(I32),
+                in_=w_words[2 * g : 2 * g + 2].rearrange("e a p n r -> p (e a) (n r)")[:, :, 4 * n0 : 4 * n1].bitcast(I32),
             )
 
-        for e in range(SPLIT_FROM):
-            load_w(e, 0, N)
+        offs_t = keep.tile([P, S // 16], U16, name="offs_t")
+        b_t = keep.tile([P, HALVES, E], F32, name="b_t")
+        load_x(0, 0, 256)
+        load_x(0, 256, T)
+        load_x(1, 0, T)
+        nc.sync.dma_start(out=offs_t[:], in_=offs)
+        load_ws(4)
+        load_x(2, 0, T)
+        load_x(3, 0, T)
+        load_ws(1)
+        load_w(0, 0, N)
+        load_ws(5)
+        load_w(1, 0, N)
+        load_ws(6)
+        load_w(2, 0, N)
+        nc.sync.dma_start(out=b_t[:], in_=b.rearrange("(h p) e -> p h e", h=HALVES))
+        load_w(3, 0, N)
         pos_t = []
         for r, pos in enumerate((pos1, pos2, pos3, pos4)):
             tile = keep.tile([P, T // 16], U16, name=f"pos_t{r}")
             nc.sync.dma_start(out=tile[:], in_=pos)
             pos_t.append(tile)
-        gate_t = keep.tile([P, R, T], F32, name="gate_t")
-        nc.sync.dma_start(out=gate_t[:], in_=gate[:, 0:P, :].rearrange("r p t -> p r t"))
         for h in range(HALVES):
-            for e in range(SPLIT_FROM, E):
-                load_w(e, h * P, (h + 1) * P)
-
-        warm = keep.tile([P, 1], F32, name="warm")
-        warm_out = keep.tile([P, 1], F32, name="warm_out")
-        nc.vector.memset(warm[:], 0.0)
-        nc.scalar.activation(out=warm_out[:], in_=warm[:], func=IDENT)
+            for g in (4, 5):
+                load_w(g, h * P, (h + 1) * P)
 
         codes = []
         for a in range(PASSES):
-            codes.append(keep.tile([P, WINDOW], U32, name=f"codes{a}", align_bytes=64))
-            nc.vector.memset(codes[a][:, T:WINDOW].bitcast(I32), 0)
+            width = WINDOW if a < 3 else WINDOW // 2
+            codes.append(keep.tile([P, width], U32, name=f"codes{a}", align_bytes=64))
         scales = keep.tile([P, WINDOW], U8, name="scales", align_bytes=64)
-        nc.gpsimd.memset(scales[:], 0)
+        nc.vector.memset(scales[:, 0:T].bitcast(I32), 0)
 
         slot_codes = []
         for a in range(PASSES):
@@ -127,29 +145,40 @@ def tile_moe_tk_lin_bias_kernel(tc, xT, w_words, w_scales, b, gate, offs, pos1, 
             cast(nc.scalar.copy, a, 0, T)
         for a in (0, 1):
             quantise(a)
-            gather(slot_codes[a], codes[a], 0, S // 2)
-            gather(slot_codes[a], codes[a], S // 2, S)
+            gather(slot_codes[a], codes[a], 0, S)
         quantise(2)
+        gather(slot_codes[2], codes[2], 0, S)
         quantise(3)
-        gather(slot_scales, scales, 0, S // 2)
-        gather(slot_scales, scales, S // 2, S)
+        gather(slot_scales, scales, 0, S)
+
+        gate_psum = psum.tile([P, 512], F32, name="gate_psum", tag="bank1_2")
+        for t in range(T // P):
+            nc.tensor.transpose(gate_psum[:, t * P : (t + 1) * P], gate_rows[:, t * P : (t + 1) * P], ident[:])
+        gate_col = keep.tile([P, T // P, R], F32, name="gate_col")
+        nc.scalar.copy(out=gate_col[:], in_=gate_psum[:, 0:T].rearrange("p (t c) -> p t c", c=P)[:, :, 0:R])
+        gate_t = keep.tile([P, R, T], F32, name="gate_t")
+        for r, tag in enumerate(("bank0_3", "bank0_4", "bank1_0", "bank1_1")):
+            spread = psum.tile([P, 512], F32, name=f"spread{r}", tag=tag)
+            for t in range(T // P):
+                nc.tensor.transpose(spread[:, t * P : (t + 1) * P], gate_col[:, t, r : r + 1].to_broadcast([P, P]), ident[:])
+            nc.scalar.copy(out=gate_t[:, r, :], in_=spread[:, 0:T])
 
         y = []
         for h in range(HALVES):
             y.append(keep.tile([P, S], F32, name=f"y{h}"))
         bank0 = []
         for c in range(len(CHUNKS)):
-            bank0.append(psum.tile([P, 512], F32, name=f"bank0_{c}"))
+            bank0.append(psum.tile([P, 512], F32, name=f"bank0_{c}", tag=f"bank0_{c}"))
         bank1 = []
         for c in range(3):
-            bank1.append(psum.tile([P, 512], F32, name=f"bank1_{c}"))
+            bank1.append(psum.tile([P, 512], F32, name=f"bank1_{c}", tag=f"bank1_{c}"))
 
         def multiply(e, h, bank, col):
             for a in range(PASSES):
-                n0 = a * N + h * P
+                n0 = (e % 2 * PASSES + a) * N + h * P
                 nc.tensor.matmul_mx(
                     out=bank[:, col : col + C],
-                    lhsT=w_t[e][:, n0 : n0 + P].bitcast(FP8X4),
+                    lhsT=w_t[e // 2][:, n0 : n0 + P].bitcast(FP8X4),
                     lhsT_scale=ws[4 * a : P, e * N + h * P : e * N + (h + 1) * P],
                     rhs=slot_codes[a][:, e * C : (e + 1) * C].bitcast(FP8X4),
                     rhs_scale=slot_scales[4 * a : P, e * C : (e + 1) * C],
@@ -161,13 +190,12 @@ def tile_moe_tk_lin_bias_kernel(tc, xT, w_words, w_scales, b, gate, offs, pos1, 
             nc.scalar.activation(out=y[h][:, e * C : (e + 1) * C], in_=bank[:, col : col + C], func=IDENT, bias=b_t[:, h, e : e + 1])
 
         for c, (e0, e1) in enumerate(CHUNKS):
-            for a in (2, 3):
-                gather(slot_codes[a], codes[a], e0 * C, e1 * C)
+            gather(slot_codes[3], codes[3], e0 * C, e1 * C)
             for e in range(e0, e1):
                 multiply(e, 0, bank0[c], (e - e0) * C)
             for e in range(e0, e1):
                 take_out(e, 0, bank0[c], (e - e0) * C)
-            for e in range(e0, e1):
+            for e in SECOND[c]:
                 multiply(e, 1, bank1[e // 4], (e % 4) * C)
                 if e % 4 == 3:
                     for f in range(e - 3, e + 1):
@@ -180,14 +208,28 @@ def tile_moe_tk_lin_bias_kernel(tc, xT, w_words, w_scales, b, gate, offs, pos1, 
         def fetch(h, r):
             nc.vector.tensor_tensor(prod[h][:, r, :], y[h][:].indirect(pos_t[r][:]), gate_t[:, r, :], MULT)
 
-        pair, res = [], []
+        acc = []
         for h in range(HALVES):
-            pair.append(keep.tile([P, 2, T], F32, name=f"pair{h}"))
-            res.append(keep.tile([P, T], F32, name=f"res{h}"))
-        for h in range(HALVES):
-            for r in range(R):
-                fetch(h, r)
-            for u in range(2):
-                nc.vector.tensor_tensor(out=pair[h][:, u, :], in0=prod[h][:, 2 * u, :], in1=prod[h][:, 2 * u + 1, :], op=ADD)
-            nc.vector.tensor_tensor(out=res[h][:], in0=pair[h][:, 0, :], in1=pair[h][:, 1, :], op=ADD)
-            nc.sync.dma_start(out=out[h * P : (h + 1) * P, :], in_=res[h][:])
+            acc.append(keep.tile([P, R - 1, T], F32, name=f"acc{h}"))
+
+        def add(h, r):
+            first = prod[h][:, 0, :] if r == 1 else acc[h][:, r - 2, :]
+            nc.vector.tensor_tensor(out=acc[h][:, r - 1, :], in0=first, in1=prod[h][:, r, :], op=ADD)
+
+        def store(h):
+            nc.sync.dma_start(out=out[h * P : (h + 1) * P, :], in_=acc[h][:, R - 2, :])
+
+        for r in range(R):
+            fetch(0, r)
+        add(0, 1)
+        fetch(1, 0)
+        add(0, 2)
+        fetch(1, 1)
+        add(0, 3)
+        store(0)
+        fetch(1, 2)
+        add(1, 1)
+        fetch(1, 3)
+        add(1, 2)
+        add(1, 3)
+        store(1)

from contextlib import ExitStack

import concourse.mybir as mybir
from concourse.masks import make_identity

K, T, E, C, N, R = 2048, 384, 12, 128, 256, 4
S = E * C
P = 128
PASSES = 4
HALVES = 2
WINDOW = 2048

FLOPS = 2 * S * K * N
BYTES = 4 * K * T + E * K * N + E * K * N // 32 + 4 * N * E + 4 * R * T + 2 * P * (S + R * T) // 16 + 4 * N * T

F32 = mybir.dt.float32
BF16 = mybir.dt.bfloat16
U32 = mybir.dt.uint32
I32 = mybir.dt.int32
U16 = mybir.dt.uint16
U8 = mybir.dt.uint8
FP8X4 = mybir.dt.float8_e4m3fn_x4

IDENT = mybir.ActivationFunctionType.Identity
MULT = mybir.AluOpType.mult
ADD = mybir.AluOpType.add

SECOND = ((), (), (), (), (0, 1, 2, 3, 4, 5, 6, 7, 8, 9, 10, 11))
CHUNKS = ((0, 3), (3, 6), (6, 9), (9, 11), (11, 12))


def tile_moe_tk_lin_bias_kernel(tc, xT, w_words, w_scales, b, gate, offs, pos1, pos2, pos3, pos4, out):
    nc = tc.nc
    with ExitStack() as ctx:
        keep = ctx.enter_context(tc.tile_pool(name="keep", bufs=1))
        psum = ctx.enter_context(tc.psum_pool(name="psum", bufs=1))

        warm = keep.tile([P, 1], F32, name="warm")
        warm_out = keep.tile([P, 1], F32, name="warm_out")
        nc.vector.memset(warm[:], 0.0)
        nc.scalar.activation(out=warm_out[:], in_=warm[:], func=IDENT)
        ws = keep.tile([P, E * N], U8, name="ws", align_bytes=64)
        nc.vector.memset(ws[:].bitcast(I32), 0)
        gate_rows = keep.tile([P, T], F32, name="gate_rows")
        nc.gpsimd.memset(gate_rows[:], 0.0)
        nc.gpsimd.dma_start(out=gate_rows[0:R, :], in_=gate[:, 0, :])
        ident = keep.tile([P, P], F32, name="ident")
        make_identity(nc, ident[:])

        x_parts = []
        for a in range(PASSES):
            x_parts.append([])

        def load_x(a, t0, t1):
            raw = keep.tile([P, 4, t1 - t0], F32, name=f"raw{a}_{t0}")
            nc.sync.dma_start(out=raw[:], in_=xT[512 * a : 512 * (a + 1), t0:t1].rearrange("(p j) t -> p j t", j=4))
            x_parts[a].append((t0, t1, raw))

        small = []
        for q in range(4):
            for a in range(PASSES):
                small.append((q, a))

        def load_ws(count):
            for u in range(count):
                q, a = small.pop(0)
                row = 32 * q + 4 * a
                nc.sync.dma_start(
                    out=ws[row : row + 4, :].rearrange("r (e n) -> r e n", e=E).bitcast(I32),
                    in_=w_scales[:, a, 4 * q : 4 * q + 4, :].rearrange("e r n -> r e n").bitcast(I32),
                )

        w_t = []
        for g in range(E // 2):
            w_t.append(keep.tile([P, 2 * PASSES * N], U32, name=f"w{g}", align_bytes=64))

        def load_w(g, n0, n1):
            nc.sync.dma_start(
                out=w_t[g][:].rearrange("p (a n) -> p a n", a=2 * PASSES)[:, :, n0:n1].bitcast(I32),
                in_=w_words[2 * g : 2 * g + 2].rearrange("e a p n r -> p (e a) (n r)")[:, :, 4 * n0 : 4 * n1].bitcast(I32),
            )

        offs_t = keep.tile([P, S // 16], U16, name="offs_t")
        b_t = keep.tile([P, HALVES, E], F32, name="b_t")
        load_x(0, 0, 256)
        load_x(0, 256, T)
        load_x(1, 0, T)
        nc.sync.dma_start(out=offs_t[:], in_=offs)
        load_ws(4)
        load_x(2, 0, T)
        load_x(3, 0, T)
        load_ws(1)
        load_w(0, 0, N)
        load_ws(5)
        load_w(1, 0, N)
        load_ws(6)
        load_w(2, 0, N)
        nc.sync.dma_start(out=b_t[:], in_=b.rearrange("(h p) e -> p h e", h=HALVES))
        load_w(3, 0, N)
        pos_t = []
        for r, pos in enumerate((pos1, pos2, pos3, pos4)):
            tile = keep.tile([P, T // 16], U16, name=f"pos_t{r}")
            nc.sync.dma_start(out=tile[:], in_=pos)
            pos_t.append(tile)
        for h in range(HALVES):
            for g in (4, 5):
                load_w(g, h * P, (h + 1) * P)

        codes = []
        for a in range(PASSES):
            width = WINDOW if a < 3 else WINDOW // 2
            codes.append(keep.tile([P, width], U32, name=f"codes{a}", align_bytes=64))
        scales = keep.tile([P, WINDOW], U8, name="scales", align_bytes=64)
        nc.vector.memset(scales[:, 0:T].bitcast(I32), 0)

        slot_codes = []
        for a in range(PASSES):
            slot_codes.append(keep.tile([P, S], U32, name=f"slot_codes{a}", align_bytes=64))
        slot_scales = keep.tile([P, S], U8, name="slot_scales", align_bytes=64)

        grouped = []
        for a in range(PASSES):
            grouped.append(keep.tile([P, T, 4], BF16, name=f"grouped{a}", align_bytes=64))

        def cast(engine_copy, a, t0, t1):
            for p0, p1, raw in x_parts[a]:
                if p0 <= t0 and t1 <= p1:
                    engine_copy(out=grouped[a][:, t0:t1, :], in_=raw[:, :, t0 - p0 : t1 - p0].rearrange("p j t -> p t j"))

        def quantise(a):
            for t0, t1 in ((0, 256), (256, 384)):
                nc.vector.quantize_mx(
                    out=codes[a][:, t0:t1].bitcast(FP8X4),
                    scales=scales[4 * a : P, t0:t1],
                    in_=grouped[a][:, t0:t1, :].rearrange("p t j -> p (t j)"),
                )

        def gather(dst, src, s0, s1):
            nc.vector.tensor_copy(dst[:, s0:s1], src[:].indirect(offs_t[:, s0 // 16 : s1 // 16]))

        cast(nc.vector.tensor_copy, 0, 0, 128)
        cast(nc.scalar.copy, 0, 128, 256)
        cast(nc.vector.tensor_copy, 0, 256, 384)
        for a in range(1, PASSES):
            cast(nc.scalar.copy, a, 0, T)
        for a in (0, 1):
            quantise(a)
            gather(slot_codes[a], codes[a], 0, S)
        quantise(2)
        gather(slot_codes[2], codes[2], 0, S)
        quantise(3)
        gather(slot_scales, scales, 0, S)

        gate_psum = psum.tile([P, 512], F32, name="gate_psum", tag="bank1_2")
        for t in range(T // P):
            nc.tensor.transpose(gate_psum[:, t * P : (t + 1) * P], gate_rows[:, t * P : (t + 1) * P], ident[:])
        gate_col = keep.tile([P, T // P, R], F32, name="gate_col")
        nc.scalar.copy(out=gate_col[:], in_=gate_psum[:, 0:T].rearrange("p (t c) -> p t c", c=P)[:, :, 0:R])
        gate_t = keep.tile([P, R, T], F32, name="gate_t")
        for r, tag in enumerate(("bank0_3", "bank0_4", "bank1_0", "bank1_1")):
            spread = psum.tile([P, 512], F32, name=f"spread{r}", tag=tag)
            for t in range(T // P):
                nc.tensor.transpose(spread[:, t * P : (t + 1) * P], gate_col[:, t, r : r + 1].to_broadcast([P, P]), ident[:])
            nc.scalar.copy(out=gate_t[:, r, :], in_=spread[:, 0:T])

        y = []
        for h in range(HALVES):
            y.append(keep.tile([P, S], F32, name=f"y{h}"))
        bank0 = []
        for c in range(len(CHUNKS)):
            bank0.append(psum.tile([P, 512], F32, name=f"bank0_{c}", tag=f"bank0_{c}"))
        bank1 = []
        for c in range(3):
            bank1.append(psum.tile([P, 512], F32, name=f"bank1_{c}", tag=f"bank1_{c}"))

        def multiply(e, h, bank, col):
            for a in range(PASSES):
                n0 = (e % 2 * PASSES + a) * N + h * P
                nc.tensor.matmul_mx(
                    out=bank[:, col : col + C],
                    lhsT=w_t[e // 2][:, n0 : n0 + P].bitcast(FP8X4),
                    lhsT_scale=ws[4 * a : P, e * N + h * P : e * N + (h + 1) * P],
                    rhs=slot_codes[a][:, e * C : (e + 1) * C].bitcast(FP8X4),
                    rhs_scale=slot_scales[4 * a : P, e * C : (e + 1) * C],
                    start=(a == 0),
                    stop=(a == PASSES - 1),
                )

        def take_out(e, h, bank, col):
            nc.scalar.activation(out=y[h][:, e * C : (e + 1) * C], in_=bank[:, col : col + C], func=IDENT, bias=b_t[:, h, e : e + 1])

        for c, (e0, e1) in enumerate(CHUNKS):
            gather(slot_codes[3], codes[3], e0 * C, e1 * C)
            for e in range(e0, e1):
                multiply(e, 0, bank0[c], (e - e0) * C)
            for e in range(e0, e1):
                take_out(e, 0, bank0[c], (e - e0) * C)
            for e in SECOND[c]:
                multiply(e, 1, bank1[e // 4], (e % 4) * C)
                if e % 4 == 3:
                    for f in range(e - 3, e + 1):
                        take_out(f, 1, bank1[f // 4], (f % 4) * C)

        prod = []
        for h in range(HALVES):
            prod.append(keep.tile([P, R, T], F32, name=f"prod{h}"))

        def fetch(h, r):
            nc.vector.tensor_tensor(prod[h][:, r, :], y[h][:].indirect(pos_t[r][:]), gate_t[:, r, :], MULT)

        acc = []
        for h in range(HALVES):
            acc.append(keep.tile([P, R - 1, T], F32, name=f"acc{h}"))

        def add(h, r):
            first = prod[h][:, 0, :] if r == 1 else acc[h][:, r - 2, :]
            nc.vector.tensor_tensor(out=acc[h][:, r - 1, :], in0=first, in1=prod[h][:, r, :], op=ADD)

        def store(h):
            nc.sync.dma_start(out=out[h * P : (h + 1) * P, :], in_=acc[h][:, R - 2, :])

        for r in range(R):
            fetch(0, r)
        add(0, 1)
        fetch(1, 0)
        add(0, 2)
        fetch(1, 1)
        add(0, 3)
        store(0)
        fetch(1, 2)
        add(1, 1)
        fetch(1, 3)
        add(1, 2)
        add(1, 3)
        store(1)
